import numpy as np
import ml_dtypes


def mxq(x, axis, fmt="e4m3"):
    dtype, down = {"e4m3": (ml_dtypes.float8_e4m3fn, 7), "e5m2": (ml_dtypes.float8_e5m2, 14)}[fmt]
    v = np.moveaxis(np.asarray(x, np.float32).astype(ml_dtypes.bfloat16).astype(np.float64), axis, -1)
    blocks = v.reshape(v.shape[:-1] + (-1, 32))
    amax = np.abs(blocks).max(-1, keepdims=True)
    byte = np.maximum(np.where(amax > 0, np.frexp(amax)[1] - 1 + 127, 0) - down, 1)
    scale = np.exp2(byte - 127.0)
    codes = (blocks / scale).astype(np.float32).astype(dtype).astype(np.float64)
    return np.moveaxis((codes * scale).reshape(v.shape), -1, axis)


WIDE = False


def mx_kscale(k):
    if not WIDE:
        return np.ones(k)
    levels = np.array([10, -10, 5, -5, 0])
    if k % 512:
        return np.exp2(np.random.permutation(np.resize(levels, k // 32))).repeat(32)
    a = np.empty((k // 512, 16))
    for p in range(k // 512):
        a[p, :8] = np.random.permutation(np.resize(levels, 8))
        for g in range(8):
            far = levels[np.abs(levels - a[p, g]) >= 10]
            a[p, g + 8] = far[np.random.randint(len(far))]
    return np.exp2(a.ravel()).repeat(32)


def f64(x):
    return np.asarray(x).astype(np.float64)


def striped(idx):
    return np.tile(idx.reshape(-1, 16).T, (8, 1)).astype(np.uint16)


def unstriped(offs):
    return offs[:16].T.reshape(-1).astype(np.int64)


def striped8(idx):
    return np.concatenate([x.reshape(-1, 16).T for x in idx]).astype(np.uint16)


def runs(offs, k):
    lists = np.stack([offs[16 * r : 16 * r + 16].T.reshape(-1) for r in range(8)]).astype(np.int64)
    return lists[np.arange(k) % 512 // 64]


def pack_weight(w):
    k, n = w.shape
    w = f64(np.asarray(w, np.float32).astype(ml_dtypes.bfloat16)).reshape(k // 32, 32, n)
    amax = np.abs(w).max(1)
    byte = np.clip(np.where(amax > 0, np.frexp(amax)[1] - 1 + 127 - 7, 1), 1, 254)
    scaled = (w * np.exp2(127.0 - byte)[:, None, :]).reshape(k, n).astype(np.float32)
    words = np.ascontiguousarray(scaled.reshape(k // 512, 128, 4, n).transpose(0, 1, 3, 2)).astype(ml_dtypes.float8_e4m3fn).view(np.uint8)
    return words, np.ascontiguousarray(byte.astype(np.uint8).reshape(k // 512, 16, n))


def unpack_weight(words, scales):
    g, p, n, _ = words.shape
    vals = np.ascontiguousarray(words).view(ml_dtypes.float8_e4m3fn).astype(np.float64) * np.repeat(np.exp2(scales.astype(np.float64) - 127.0), 8, axis=1)[..., None]
    return vals.transpose(0, 1, 3, 2).reshape(g * 512, n)


K, T, S, V, H, W = 512, 2048, 512, 512, 512, 256


def setup_inputs():
    n = np.random.standard_normal
    s = mx_kscale(K)[:, None]
    u = mx_kscale(S)
    packed_xT = pack_weight(n((K, T)) * s)
    perm = np.stack([np.random.permutation(S) for _ in range(8)])
    return {
        "x_words": packed_xT[0],
        "x_scales": packed_xT[1],
        "w1": (n((K, H)) / np.sqrt(K) / s).astype(np.float32),
        "w2": (n((K, H)) / np.sqrt(K) / s).astype(np.float32),
        "ga": (np.random.uniform(0.5, 1.5, (H, 1)) * u[:, None]).astype(np.float32),
        "gb": (np.random.uniform(0.5, 1.5, (H, 1)) / u[:, None]).astype(np.float32),
        "offs": striped(np.random.permutation(T)[:S]),
        "two": striped(np.random.permutation(T)[:V]),
        "n1": striped8(perm[:, :W]),
        "n2": striped8(perm[:, W:]),
        "n3": striped8(np.stack([np.random.permutation(V) for _ in range(8)])),
        "n4": striped8(np.stack([np.random.permutation(V) for _ in range(8)])),
        "n5": striped8(np.stack([np.random.permutation(V) for _ in range(8)])),
        "n6": striped8(np.stack([np.random.permutation(V) for _ in range(8)])),
        "n7": striped8(np.stack([np.random.permutation(V) for _ in range(8)])),
        "n8": striped8(np.stack([np.random.permutation(V) for _ in range(8)])),
    }


def reference(x_words, x_scales, w1, w2, ga, gb, offs, two, n1, n2, n3, n4, n5, n6, n7, n8):
    xq = unpack_weight(x_words, x_scales)[:, unstriped(offs)]
    a = mxq(f64(w1), 0, "e4m3").T @ xq
    pa = a[np.arange(H)[:, None], runs(n1, H)]
    pb = a[np.arange(H)[:, None], runs(n2, H)]
    rb = np.maximum(0.5 * pa, pb)
    ra = pb - pa
    ds = np.zeros((H, S))
    ds[np.arange(H)[:, None], runs(n1, H)] = ra
    dt = ds.copy()
    dt[np.arange(H)[:, None], runs(n2, H)] = rb
    z = f64(ga) * dt
    x_two = unpack_weight(x_words, x_scales)[:, unstriped(two)]
    b = mxq(f64(w2), 0, "e4m3").T @ x_two
    st = b - (b[np.arange(H)[:, None], runs(n3, H)])
    su = np.maximum(st, st[np.arange(H)[:, None], runs(n4, H)])
    z2 = f64(gb) * (su + 0.5 * (su[np.arange(H)[:, None], runs(n5, H)]))
    s = 0.0625 * ((mxq(z, 0, "e4m3").T @ mxq(z2, 0, "e4m3")))
    ex = np.exp(0.5 * s)
    return np.log((ex + ex[np.arange(S)[:, None], runs(n6, S)]) / (ex[np.arange(S)[:, None], runs(n7, S)] + ex[np.arange(S)[:, None], runs(n8, S)]))

@@ -1,0 +1,237 @@
+from contextlib import ExitStack
+
+import concourse.mybir as mybir
+
+K, T, S, V, H, W = 512, 2048, 512, 512, 512, 256
+FLOPS = 3 * 2 * 512 * 512 * 512
+
+F32 = mybir.dt.float32
+BF16 = mybir.dt.bfloat16
+I32 = mybir.dt.int32
+U32 = mybir.dt.uint32
+U16 = mybir.dt.uint16
+U8 = mybir.dt.uint8
+FP8X4 = mybir.dt.float8_e4m3fn_x4
+ALU = mybir.AluOpType
+ACT = mybir.ActivationFunctionType
+
+P = 128
+PACK = 4
+HALF = 256
+BIG = 3.0e38
+SPLIT = 64
+
+
+def tile_picked_kqliftthreeodds_none_p_kernel(tc, x_words, x_scales, w1, w2, ga, gb, offs, two, n1, n2, n3, n4, n5, n6, n7, n8, out):
+    nc = tc.nc
+    with ExitStack() as ctx:
+        keep = ctx.enter_context(tc.tile_pool(name="keep", bufs=1))
+        turn = ctx.enter_context(tc.tile_pool(name="turn", bufs=1))
+        psum = ctx.enter_context(tc.psum_pool(name="psum", bufs=1))
+
+        def sb(name, shape, dtype, tag=None):
+            return keep.tile(shape, dtype, name=name, tag=tag or name, align_bytes=64)
+
+        def per_tile(name, width):
+            return [sb(f"{name}{t}", [P, width], F32) for t in range(PACK)]
+
+        def load_list(name, src):
+            tile = sb(name, list(src.shape), U16)
+            nc.sync.dma_start(tile[:], src)
+            return tile
+
+        def load_weight_half(name, w, half):
+            tile = sb(name, [P, PACK, HALF], F32)
+            nc.sync.dma_start(tile[:], w.rearrange("(p j) c -> p j c", j=PACK)[:, :, half * HALF : (half + 1) * HALF])
+            return tile
+
+        xs = sb("xs", [P, T], U8)
+        nc.gpsimd.memset(xs[:].bitcast(I32), 0)
+        l_offs = load_list("l_offs", offs)
+        l_two = load_list("l_two", two)
+        w1_raw = [load_weight_half("w1_raw0", w1, 0)]
+        for q in range(4):
+            nc.sync.dma_start(xs[32 * q : 32 * q + 4, :].bitcast(I32), x_scales[0, 4 * q : 4 * q + 4, :].bitcast(I32))
+        w1_raw.append(load_weight_half("w1_raw1", w1, 1))
+        xw = sb("xw", [P, T], U32)
+        nc.sync.dma_start(xw[:].bitcast(I32), x_words[0].rearrange("p n t -> p (n t)").bitcast(I32))
+        ga_sb = sb("ga_sb", [P, PACK], F32)
+        gb_sb = sb("gb_sb", [P, PACK], F32)
+        nc.sync.dma_start(ga_sb[:], ga.rearrange("(p t) o -> p (t o)", t=PACK))
+        nc.sync.dma_start(gb_sb[:], gb.rearrange("(p t) o -> p (t o)", t=PACK))
+        l1 = load_list("l1", n1)
+        l2 = load_list("l2", n2)
+        w2_raw = [load_weight_half(f"w2_raw{h}", w2, h) for h in range(2)]
+        l3 = load_list("l3", n3)
+        l4 = load_list("l4", n4)
+        l5 = load_list("l5", n5)
+        l6 = load_list("l6", n6)
+        l7 = load_list("l7", n7)
+        l8 = load_list("l8", n8)
+
+        neg_b = sb("neg_b", [P, PACK], F32)
+        sign_b = sb("sign_b", [P, PACK], F32)
+        gain_a = sb("gain_a", [P, PACK], F32)
+        gain_b = sb("gain_b", [P, PACK], F32)
+        low = sb("low", [P, PACK], F32)
+        high = sb("high", [P, PACK], F32)
+        nc.gpsimd.tensor_scalar(neg_b[:], gb_sb[:], 0.0, -2.0, ALU.is_lt, ALU.mult)
+        nc.gpsimd.tensor_scalar(sign_b[:], neg_b[:], 1.0, 1.0, ALU.mult, ALU.add)
+        nc.gpsimd.tensor_tensor(gain_a[:], ga_sb[:], sign_b[:], ALU.mult)
+        nc.gpsimd.tensor_tensor(gain_b[:], gb_sb[:], sign_b[:], ALU.mult)
+        nc.gpsimd.tensor_scalar(high[:], gain_a[:], 0.0, BIG, ALU.is_ge, ALU.mult)
+        nc.gpsimd.tensor_scalar(low[:], gain_a[:], 0.0, -BIG, ALU.is_lt, ALU.mult)
+
+        xa_s = sb("xa_s", [P, S], U8)
+        xb_s = sb("xb_s", [P, V], U8)
+        xa_w = sb("xa_w", [P, S], U32)
+        xb_w = sb("xb_w", [P, V], U32)
+        nc.vector.tensor_copy(xa_s[:], xs[:].indirect(l_offs[:]))
+        nc.vector.tensor_copy(xb_s[:], xs[:].indirect(l_two[:]))
+        nc.vector.tensor_copy(xa_w[:], xw[:].indirect(l_offs[:]))
+
+        def quantise(name, grouped, pieces):
+            codes = sb(name + "_w", [P, 512], U32)
+            scales = sb(name + "_s", [P, 512], U8)
+            n = 512 // pieces
+            steps = []
+            for i in range(pieces):
+                steps.append(lambda i=i: nc.vector.quantize_mx(
+                    out=codes[:, i * n : (i + 1) * n].bitcast(FP8X4),
+                    scales=scales[:, i * n : (i + 1) * n],
+                    in_=grouped[:, PACK * i * n : PACK * (i + 1) * n]))
+            return codes, scales, steps
+
+        def weight(name, raw, cast, grouped, pieces):
+            dst = grouped[:].rearrange("p (t m j) -> p m j t", t=PACK, j=PACK)
+            for h in range(2):
+                cast(dst[:, 64 * h : 64 * (h + 1)], raw[h][:].rearrange("p j (m t) -> p m j t", t=PACK))
+            codes, scales, steps = quantise(name, grouped, pieces)
+            for step in steps:
+                step()
+            return codes, scales
+
+        def product(bank, lw, ls, t, rw, rs):
+            nc.tensor.matmul_mx(out=bank[:], lhsT=lw[:, t * P : (t + 1) * P].bitcast(FP8X4), lhsT_scale=ls[:, t * P : (t + 1) * P],
+                                rhs=rw[:].bitcast(FP8X4), rhs_scale=rs[:], start=True, stop=True)
+
+        w1_w, w1_s = weight("w1q", w1_raw, lambda dst, src: nc.scalar.activation(dst, src, ACT.Copy), sb("w1_g", [P, 2048], BF16), 4)
+        a_ps = [psum.tile([P, 512], F32, name=f"a_ps{t}", tag=f"last{t}") for t in range(PACK)]
+        for t in range(PACK):
+            product(a_ps[t], w1_w, w1_s, t, xa_w, xa_s)
+        nc.vector.tensor_copy(xb_w[:], xw[:].indirect(l_two[:]))
+        w2_w, w2_s = weight("w2q", w2_raw, nc.vector.tensor_copy, turn.tile([P, 2048], BF16, name="w2_g", align_bytes=64, offset=0), 1)
+
+        b_ps = [psum.tile([P, 512], F32, name=f"b_ps{t}") for t in range(PACK)]
+        for t in range(PACK):
+            product(b_ps[t], w2_w, w2_s, t, xb_w, xb_s)
+        a_sb = per_tile("a_sb", 512)
+        npa = per_tile("npa", W)
+        pb = per_tile("pb", W)
+        gap = per_tile("gap", W)
+        z_all = sb("z_all", [P, PACK, 512], F32)
+        b_sb = per_tile("b_sb", 512)
+        st = per_tile("st", 1024)
+        su = per_tile("su", 1024)
+        su_all = sb("su_all", [P, PACK, 512], F32)
+        h5_all = sb("h5_all", [P, PACK, 512], F32)
+
+        def leave_a(t):
+            nc.scalar.activation(a_sb[t][:], a_ps[t][:], ACT.Copy, scale=gain_a[:, t : t + 1])
+
+        def leave_b(t):
+            nc.scalar.activation(b_sb[t][:], b_ps[t][:], ACT.Copy, scale=gain_b[:, t : t + 1])
+
+        def pair_fetch(t):
+            nc.scalar.activation(npa[t][:], a_sb[t][:].indirect(l1[:]), ACT.Copy, scale=-1.0)
+            nc.scalar.activation(pb[t][:], a_sb[t][:].indirect(l2[:]), ACT.Copy)
+            nc.vector.scalar_tensor_tensor(gap[t][:], npa[t][:], -0.5, pb[t][:], ALU.mult, ALU.subtract)
+
+        def put_first(t, dt):
+            nc.vector.tensor_tensor(dt[:].indirect(l1[:]), pb[t][:], npa[t][:], ALU.add)
+            return dt
+
+        def put_second(t, dt, tag):
+            lift = sb(f"lift{t}", [P, W], F32, tag)
+            nc.vector.tensor_scalar(lift[:], gap[t][:], low[:, t : t + 1], high[:, t : t + 1], ALU.max, ALU.min)
+            nc.vector.tensor_tensor(dt[:].indirect(l2[:]), pb[t][:], lift[:], ALU.add)
+            if t < PACK - 1:
+                nc.sync.dma_start(z_all[:, t, :], dt[:])
+            else:
+                nc.vector.tensor_copy(z_all[:, t, :], dt[:])
+
+        def diff_stage(t):
+            for h in range(2):
+                nc.scalar.activation(st[t][:, 512 + h * HALF : 512 + (h + 1) * HALF], b_sb[t][:].indirect(l3[:, 16 * h : 16 * h + 16]), ACT.Copy)
+            nc.vector.tensor_tensor(st[t][:, 0:512], b_sb[t][:], st[t][:, 512:1024], ALU.subtract)
+
+        def max_stage(t):
+            nc.scalar.activation(su[t][:, 512:1024], st[t][:].indirect(l4[:]), ACT.Copy)
+            nc.vector.tensor_tensor(su[t][:, 0:512], st[t][:, 0:512], su[t][:, 512:1024], ALU.max)
+            nc.sync.dma_start(su_all[:, t, :], su[t][:, 0:512])
+
+        early = [turn.tile([P, 512], F32, name=f"dt{t}", align_bytes=64, offset=2048 * t) for t in range(PACK - 1)]
+        leave_a(0)
+        for t in range(PACK - 1):
+            leave_a(t + 1)
+            pair_fetch(t)
+            put_second(t, put_first(t, early[t]), None)
+        leave_b(0)
+        pair_fetch(PACK - 1)
+        for t in range(PACK):
+            if t + 1 < PACK:
+                leave_b(t + 1)
+            diff_stage(t)
+        max_stage(0)
+        dt_last = put_first(PACK - 1, sb("dt3", [P, 512], F32, "st0"))
+        for t in range(1, PACK):
+            max_stage(t)
+        put_second(PACK - 1, dt_last, "st3")
+
+        z2_g = sb("z2_g", [P, 2048], BF16)
+        z2_w, z2_s, z2_steps = quantise("z2q", z2_g, 2)
+        z_g = sb("z_g", [P, 2048], BF16)
+        z_w, z_s, z_steps = quantise("zq", z_g, 1)
+
+        def sum_stage(h):
+            cols = slice(h * HALF, (h + 1) * HALF)
+            for t in range(PACK):
+                nc.scalar.activation(h5_all[:, t, cols], su[t][:].indirect(l5[:, 16 * h : 16 * h + 16]), ACT.Copy, scale=0.5)
+            nc.vector.tensor_tensor(
+                z2_g[:, PACK * h * HALF : PACK * (h + 1) * HALF].rearrange("p (c i t) -> p c t i", i=4, t=PACK),
+                su_all[:, :, cols].rearrange("p t (c i) -> p c t i", i=4),
+                h5_all[:, :, cols].rearrange("p t (c i) -> p c t i", i=4),
+                ALU.add)
+            z2_steps[h]()
+
+        z_dst = z_g[:].rearrange("p (u m t) -> p m t u", u=PACK, t=PACK)
+        z_src = z_all[:].rearrange("p t (m u) -> p m t u", u=PACK)
+        nc.vector.tensor_copy(z_dst[:, 0:SPLIT], z_src[:, 0:SPLIT])
+        sum_stage(0)
+        sum_stage(1)
+        nc.scalar.copy(z_dst[:, SPLIT:128], z_src[:, SPLIT:128])
+        z_steps[0]()
+
+        s_ps = [psum.tile([P, 512], F32, name=f"s_ps{t}", tag=f"last{t}") for t in range(PACK)]
+        shift = per_tile("shift", 1)
+        ex2 = per_tile("ex2", 512)
+        g7 = per_tile("g7", 512)
+        num = per_tile("num", 512)
+        den = per_tile("den", 512)
+        res = per_tile("res", 512)
+        out_rows = out.rearrange("(p u) v -> p u v", u=PACK)
+        for t in range(PACK):
+            product(s_ps[t], z_w, z_s, t, z2_w, z2_s)
+        for t in range(PACK):
+            nc.scalar.activation(shift[t][:], s_ps[t][:, 0:1], ACT.Copy, scale=-0.03125)
+            nc.scalar.activation(su[t][:, 0:512], s_ps[t][:], ACT.Exp, bias=shift[t][:], scale=0.03125)
+            nc.vector.tensor_copy(ex2[t][:], su[t][:, 0:512])
+            nc.vector.tensor_tensor(num[t][:], su[t][:].indirect(l6[:]), ex2[t][:], ALU.add)
+        for t in range(PACK):
+            nc.scalar.activation(g7[t][:], su[t][:].indirect(l7[:]), ACT.Copy)
+            nc.vector.tensor_tensor(den[t][:], su[t][:].indirect(l8[:]), g7[t][:], ALU.add)
+        for t in range(PACK):
+            nc.scalar.activation(num[t][:], num[t][:], ACT.Ln)
+            nc.scalar.activation(den[t][:], den[t][:], ACT.Ln)
+            nc.vector.tensor_tensor(res[t][:], num[t][:], den[t][:], ALU.subtract)
+            nc.sync.dma_start(out_rows[:, t, :], res[t][:])

@@ -19,7 +19,6 @@ P = 128
 PACK = 4
 HALF = 256
 BIG = 3.0e38
-SPLIT = 64
 
 
 def tile_picked_kqliftthreeodds_none_p_kernel(tc, x_words, x_scales, w1, w2, ga, gb, offs, two, n1, n2, n3, n4, n5, n6, n7, n8, out):
@@ -103,7 +102,7 @@ def tile_picked_kqliftthreeodds_none_p_kernel(tc, x_words, x_scales, w1, w2, ga,
             return codes, scales, steps
 
         def weight(name, raw, cast, grouped, pieces):
-            dst = grouped[:].rearrange("p (t m j) -> p m j t", t=PACK, j=PACK)
+            dst = grouped.rearrange("p (t m j) -> p m j t", t=PACK, j=PACK)
             for h in range(2):
                 cast(dst[:, 64 * h : 64 * (h + 1)], raw[h][:].rearrange("p j (m t) -> p m j t", t=PACK))
             codes, scales, steps = quantise(name, grouped, pieces)
@@ -115,12 +114,13 @@ def tile_picked_kqliftthreeodds_none_p_kernel(tc, x_words, x_scales, w1, w2, ga,
             nc.tensor.matmul_mx(out=bank[:], lhsT=lw[:, t * P : (t + 1) * P].bitcast(FP8X4), lhsT_scale=ls[:, t * P : (t + 1) * P],
                                 rhs=rw[:].bitcast(FP8X4), rhs_scale=rs[:], start=True, stop=True)
 
-        w1_w, w1_s = weight("w1q", w1_raw, lambda dst, src: nc.scalar.activation(dst, src, ACT.Copy), sb("w1_g", [P, 2048], BF16), 4)
+        rounded = turn.tile([P, 2, 2048], BF16, name="rounded", align_bytes=64, offset=512)
+        w1_w, w1_s = weight("w1q", w1_raw, lambda dst, src: nc.scalar.activation(dst, src, ACT.Copy), rounded[:, 0, :], 4)
         a_ps = [psum.tile([P, 512], F32, name=f"a_ps{t}", tag=f"last{t}") for t in range(PACK)]
         for t in range(PACK):
             product(a_ps[t], w1_w, w1_s, t, xa_w, xa_s)
         nc.vector.tensor_copy(xb_w[:], xw[:].indirect(l_two[:]))
-        w2_w, w2_s = weight("w2q", w2_raw, nc.vector.tensor_copy, turn.tile([P, 2048], BF16, name="w2_g", align_bytes=64, offset=0), 1)
+        w2_w, w2_s = weight("w2q", w2_raw, nc.vector.tensor_copy, rounded[:, 1, :], 1)
 
         b_ps = [psum.tile([P, 512], F32, name=f"b_ps{t}") for t in range(PACK)]
         for t in range(PACK):
@@ -128,7 +128,6 @@ def tile_picked_kqliftthreeodds_none_p_kernel(tc, x_words, x_scales, w1, w2, ga,
         a_sb = per_tile("a_sb", 512)
         npa = per_tile("npa", W)
         pb = per_tile("pb", W)
-        gap = per_tile("gap", W)
         z_all = sb("z_all", [P, PACK, 512], F32)
         b_sb = per_tile("b_sb", 512)
         st = per_tile("st", 1024)
@@ -145,15 +144,15 @@ def tile_picked_kqliftthreeodds_none_p_kernel(tc, x_words, x_scales, w1, w2, ga,
         def pair_fetch(t):
             nc.scalar.activation(npa[t][:], a_sb[t][:].indirect(l1[:]), ACT.Copy, scale=-1.0)
             nc.scalar.activation(pb[t][:], a_sb[t][:].indirect(l2[:]), ACT.Copy)
-            nc.vector.scalar_tensor_tensor(gap[t][:], npa[t][:], -0.5, pb[t][:], ALU.mult, ALU.subtract)
 
-        def put_first(t, dt):
+        def put_first(t, dt, gap):
+            nc.vector.scalar_tensor_tensor(gap[:], npa[t][:], -0.5, pb[t][:], ALU.mult, ALU.subtract)
             nc.vector.tensor_tensor(dt[:].indirect(l1[:]), pb[t][:], npa[t][:], ALU.add)
-            return dt
+            return dt, gap
 
-        def put_second(t, dt, tag):
+        def put_second(t, dt, gap, tag):
             lift = sb(f"lift{t}", [P, W], F32, tag)
-            nc.vector.tensor_scalar(lift[:], gap[t][:], low[:, t : t + 1], high[:, t : t + 1], ALU.max, ALU.min)
+            nc.vector.tensor_scalar(lift[:], gap[:], low[:, t : t + 1], high[:, t : t + 1], ALU.max, ALU.min)
             nc.vector.tensor_tensor(dt[:].indirect(l2[:]), pb[t][:], lift[:], ALU.add)
             if t < PACK - 1:
                 nc.sync.dma_start(z_all[:, t, :], dt[:])
@@ -168,14 +167,18 @@ def tile_picked_kqliftthreeodds_none_p_kernel(tc, x_words, x_scales, w1, w2, ga,
         def max_stage(t):
             nc.scalar.activation(su[t][:, 512:1024], st[t][:].indirect(l4[:]), ACT.Copy)
             nc.vector.tensor_tensor(su[t][:, 0:512], st[t][:, 0:512], su[t][:, 512:1024], ALU.max)
-            nc.sync.dma_start(su_all[:, t, :], su[t][:, 0:512])
+            if t < PACK - 1:
+                nc.sync.dma_start(su_all[:, t, :], su[t][:, 0:512])
+            else:
+                nc.vector.tensor_copy(su_all[:, t, :], su[t][:, 0:512])
 
-        early = [turn.tile([P, 512], F32, name=f"dt{t}", align_bytes=64, offset=2048 * t) for t in range(PACK - 1)]
+        early = [turn.tile([P, 512], F32, name=f"dt{t}", align_bytes=64, offset=3072 * t + 1024) for t in range(PACK - 1)]
+        early_gap = [turn.tile([P, W], F32, name=f"gap{t}", align_bytes=64, offset=3072 * t) for t in range(PACK - 1)]
         leave_a(0)
         for t in range(PACK - 1):
             leave_a(t + 1)
             pair_fetch(t)
-            put_second(t, put_first(t, early[t]), None)
+            put_second(t, *put_first(t, early[t], early_gap[t]), None)
         leave_b(0)
         pair_fetch(PACK - 1)
         for t in range(PACK):
@@ -183,15 +186,15 @@ def tile_picked_kqliftthreeodds_none_p_kernel(tc, x_words, x_scales, w1, w2, ga,
                 leave_b(t + 1)
             diff_stage(t)
         max_stage(0)
-        dt_last = put_first(PACK - 1, sb("dt3", [P, 512], F32, "st0"))
+        last = put_first(PACK - 1, sb("dt3", [P, 512], F32, "st0"), sb("gap3", [P, W], F32, "b_sb0"))
         for t in range(1, PACK):
             max_stage(t)
-        put_second(PACK - 1, dt_last, "st3")
+        put_second(PACK - 1, *last, "st3")
 
         z2_g = sb("z2_g", [P, 2048], BF16)
         z2_w, z2_s, z2_steps = quantise("z2q", z2_g, 2)
         z_g = sb("z_g", [P, 2048], BF16)
-        z_w, z_s, z_steps = quantise("zq", z_g, 1)
+        z_w, z_s, z_steps = quantise("zq", z_g, 2)
 
         def sum_stage(h):
             cols = slice(h * HALF, (h + 1) * HALF)
@@ -206,18 +209,18 @@ def tile_picked_kqliftthreeodds_none_p_kernel(tc, x_words, x_scales, w1, w2, ga,
 
         z_dst = z_g[:].rearrange("p (u m t) -> p m t u", u=PACK, t=PACK)
         z_src = z_all[:].rearrange("p t (m u) -> p m t u", u=PACK)
-        nc.vector.tensor_copy(z_dst[:, 0:SPLIT], z_src[:, 0:SPLIT])
         sum_stage(0)
         sum_stage(1)
-        nc.scalar.copy(z_dst[:, SPLIT:128], z_src[:, SPLIT:128])
+        nc.scalar.copy(z_dst[:, :, :, 0:2], z_src[:, :, :, 0:2])
         z_steps[0]()
+        nc.vector.tensor_copy(z_dst[:, :, :, 2:4], z_src[:, :, :, 2:4])
+        z_steps[1]()
 
         s_ps = [psum.tile([P, 512], F32, name=f"s_ps{t}", tag=f"last{t}") for t in range(PACK)]
         shift = per_tile("shift", 1)
         ex2 = per_tile("ex2", 512)
         g7 = per_tile("g7", 512)
         num = per_tile("num", 512)
-        den = per_tile("den", 512)
         res = per_tile("res", 512)
         out_rows = out.rearrange("(p u) v -> p u v", u=PACK)
         for t in range(PACK):
@@ -225,13 +228,31 @@ def tile_picked_kqliftthreeodds_none_p_kernel(tc, x_words, x_scales, w1, w2, ga,
         for t in range(PACK):
             nc.scalar.activation(shift[t][:], s_ps[t][:, 0:1], ACT.Copy, scale=-0.03125)
             nc.scalar.activation(su[t][:, 0:512], s_ps[t][:], ACT.Exp, bias=shift[t][:], scale=0.03125)
-            nc.vector.tensor_copy(ex2[t][:], su[t][:, 0:512])
+            if t < 2:
+                nc.vector.tensor_copy(ex2[t][:], su[t][:, 0:512])
+            else:
+                nc.sync.dma_start(ex2[t][:], su[t][:, 0:512])
             nc.vector.tensor_tensor(num[t][:], su[t][:].indirect(l6[:]), ex2[t][:], ALU.add)
-        for t in range(PACK):
+
+        def below(t, den):
             nc.scalar.activation(g7[t][:], su[t][:].indirect(l7[:]), ACT.Copy)
-            nc.vector.tensor_tensor(den[t][:], su[t][:].indirect(l8[:]), g7[t][:], ALU.add)
-        for t in range(PACK):
+            nc.vector.tensor_tensor(den[:], su[t][:].indirect(l8[:]), g7[t][:], ALU.add)
+            return den
+
+        def finish(t, den, pieces=1):
             nc.scalar.activation(num[t][:], num[t][:], ACT.Ln)
-            nc.scalar.activation(den[t][:], den[t][:], ACT.Ln)
-            nc.vector.tensor_tensor(res[t][:], num[t][:], den[t][:], ALU.subtract)
-            nc.sync.dma_start(out_rows[:, t, :], res[t][:])
+            for i in range(pieces):
+                cols = slice(i * 512 // pieces, (i + 1) * 512 // pieces)
+                nc.scalar.activation(den[:, cols], den[:, cols], ACT.Ln)
+                nc.vector.tensor_tensor(res[t][:, cols], num[t][:, cols], den[:, cols], ALU.subtract)
+                nc.sync.dma_start(out_rows[:, t, cols], res[t][:, cols])
+
+        dens = [below(t, sb(f"den{t}", [P, 512], F32)) for t in range(PACK - 1)]
+        nc.scalar.activation(g7[3][:, 0:HALF], su[3][:].indirect(l7[:, 0:16]), ACT.Copy)
+        nc.vector.tensor_copy(g7[3][:, HALF:512], su[3][:].indirect(l7[:, 16:32]))
+        finish(0, dens[0])
+        den3 = sb("den3", [P, 512], F32, "den0")
+        nc.vector.tensor_tensor(den3[:], su[3][:].indirect(l8[:]), g7[3][:], ALU.add)
+        finish(1, dens[1])
+        finish(2, dens[2])
+        finish(3, den3, 2)

@@ -2,8 +2,10 @@ from contextlib import ExitStack
 
 import concourse.mybir as mybir
 
-K, T, S, V, H, W = 512, 2048, 512, 512, 512, 256
-FLOPS = 3 * 2 * 512 * 512 * 512
+T = 2048
+N = 512
+PAIRS = 256
+FLOPS = 3 * 2 * N * N * N
 
 F32 = mybir.dt.float32
 BF16 = mybir.dt.bfloat16
@@ -17,8 +19,11 @@ ACT = mybir.ActivationFunctionType
 
 P = 128
 PACK = 4
-HALF = 256
-BIG = 3.0e38
+LAST = PACK - 1
+HALF = N // 2
+GROUP = 16
+NO_BOUND = 3.0e38
+EXP_SCALE = 0.5 * 0.0625
 
 
 def tile_picked_kqliftthreeodds_none_p_kernel(tc, x_words, x_scales, w1, w2, ga, gb, offs, two, n1, n2, n3, n4, n5, n6, n7, n8, out):
@@ -28,32 +33,38 @@ def tile_picked_kqliftthreeodds_none_p_kernel(tc, x_words, x_scales, w1, w2, ga,
         turn = ctx.enter_context(tc.tile_pool(name="turn", bufs=1))
         psum = ctx.enter_context(tc.psum_pool(name="psum", bufs=1))
 
-        def sb(name, shape, dtype, tag=None):
-            return keep.tile(shape, dtype, name=name, tag=tag or name, align_bytes=64)
+        def sb(name, shape, dtype, on=None):
+            return keep.tile(shape, dtype, name=name, tag=on or name, align_bytes=64)
 
         def per_tile(name, width):
             return [sb(f"{name}{t}", [P, width], F32) for t in range(PACK)]
+
+        def half(h):
+            return slice(h * HALF, (h + 1) * HALF)
+
+        def half_list(tile, h):
+            return tile[:, h * HALF // GROUP : (h + 1) * HALF // GROUP]
 
         def load_list(name, src):
             tile = sb(name, list(src.shape), U16)
             nc.sync.dma_start(tile[:], src)
             return tile
 
-        def load_weight_half(name, w, half):
+        def load_weight_half(name, w, h):
             tile = sb(name, [P, PACK, HALF], F32)
-            nc.sync.dma_start(tile[:], w.rearrange("(p j) c -> p j c", j=PACK)[:, :, half * HALF : (half + 1) * HALF])
+            nc.sync.dma_start(tile[:], w.rearrange("(p j) c -> p j c", j=PACK)[:, :, half(h)])
             return tile
 
-        xs = sb("xs", [P, T], U8)
-        nc.gpsimd.memset(xs[:].bitcast(I32), 0)
+        x_bytes = sb("x_bytes", [P, T], U8)
+        nc.gpsimd.memset(x_bytes[:].bitcast(I32), 0)
         l_offs = load_list("l_offs", offs)
         l_two = load_list("l_two", two)
         w1_raw = [load_weight_half("w1_raw0", w1, 0)]
         for q in range(4):
-            nc.sync.dma_start(xs[32 * q : 32 * q + 4, :].bitcast(I32), x_scales[0, 4 * q : 4 * q + 4, :].bitcast(I32))
+            nc.sync.dma_start(x_bytes[32 * q : 32 * q + 4, :].bitcast(I32), x_scales[0, 4 * q : 4 * q + 4, :].bitcast(I32))
         w1_raw.append(load_weight_half("w1_raw1", w1, 1))
-        xw = sb("xw", [P, T], U32)
-        nc.sync.dma_start(xw[:].bitcast(I32), x_words[0].rearrange("p n t -> p (n t)").bitcast(I32))
+        x_codes = sb("x_codes", [P, T], U32)
+        nc.sync.dma_start(x_codes[:].bitcast(I32), x_words[0].rearrange("p n t -> p (n t)").bitcast(I32))
         ga_sb = sb("ga_sb", [P, PACK], F32)
         gb_sb = sb("gb_sb", [P, PACK], F32)
         nc.sync.dma_start(ga_sb[:], ga.rearrange("(p t) o -> p (t o)", t=PACK))
@@ -68,72 +79,70 @@ def tile_picked_kqliftthreeodds_none_p_kernel(tc, x_words, x_scales, w1, w2, ga,
         l7 = load_list("l7", n7)
         l8 = load_list("l8", n8)
 
-        neg_b = sb("neg_b", [P, PACK], F32)
+        minus_two = sb("minus_two", [P, PACK], F32)
         sign_b = sb("sign_b", [P, PACK], F32)
         gain_a = sb("gain_a", [P, PACK], F32)
         gain_b = sb("gain_b", [P, PACK], F32)
         low = sb("low", [P, PACK], F32)
         high = sb("high", [P, PACK], F32)
-        nc.gpsimd.tensor_scalar(neg_b[:], gb_sb[:], 0.0, -2.0, ALU.is_lt, ALU.mult)
-        nc.gpsimd.tensor_scalar(sign_b[:], neg_b[:], 1.0, 1.0, ALU.mult, ALU.add)
+        nc.gpsimd.tensor_scalar(minus_two[:], gb_sb[:], 0.0, -2.0, ALU.is_lt, ALU.mult)
+        nc.gpsimd.tensor_scalar(sign_b[:], minus_two[:], 1.0, 1.0, ALU.mult, ALU.add)
         nc.gpsimd.tensor_tensor(gain_a[:], ga_sb[:], sign_b[:], ALU.mult)
         nc.gpsimd.tensor_tensor(gain_b[:], gb_sb[:], sign_b[:], ALU.mult)
-        nc.gpsimd.tensor_scalar(high[:], gain_a[:], 0.0, BIG, ALU.is_ge, ALU.mult)
-        nc.gpsimd.tensor_scalar(low[:], gain_a[:], 0.0, -BIG, ALU.is_lt, ALU.mult)
+        nc.gpsimd.tensor_scalar(high[:], gain_a[:], 0.0, NO_BOUND, ALU.is_ge, ALU.mult)
+        nc.gpsimd.tensor_scalar(low[:], gain_a[:], 0.0, -NO_BOUND, ALU.is_lt, ALU.mult)
 
-        xa_s = sb("xa_s", [P, S], U8)
-        xb_s = sb("xb_s", [P, V], U8)
-        xa_w = sb("xa_w", [P, S], U32)
-        xb_w = sb("xb_w", [P, V], U32)
-        nc.vector.tensor_copy(xa_s[:], xs[:].indirect(l_offs[:]))
-        nc.vector.tensor_copy(xb_s[:], xs[:].indirect(l_two[:]))
-        nc.vector.tensor_copy(xa_w[:], xw[:].indirect(l_offs[:]))
+        xa_bytes = sb("xa_bytes", [P, N], U8)
+        xb_bytes = sb("xb_bytes", [P, N], U8)
+        xa_codes = sb("xa_codes", [P, N], U32)
+        xb_codes = sb("xb_codes", [P, N], U32)
+        nc.vector.tensor_copy(xa_bytes[:], x_bytes[:].indirect(l_offs[:]))
+        nc.vector.tensor_copy(xb_bytes[:], x_bytes[:].indirect(l_two[:]))
+        nc.vector.tensor_copy(xa_codes[:], x_codes[:].indirect(l_offs[:]))
 
-        def quantise(name, grouped, pieces):
-            codes = sb(name + "_w", [P, 512], U32)
-            scales = sb(name + "_s", [P, 512], U8)
-            n = 512 // pieces
-            steps = []
-            for i in range(pieces):
-                steps.append(lambda i=i: nc.vector.quantize_mx(
-                    out=codes[:, i * n : (i + 1) * n].bitcast(FP8X4),
-                    scales=scales[:, i * n : (i + 1) * n],
-                    in_=grouped[:, PACK * i * n : PACK * (i + 1) * n]))
-            return codes, scales, steps
-
-        def weight(name, raw, cast, grouped, pieces):
-            dst = grouped.rearrange("p (t m j) -> p m j t", t=PACK, j=PACK)
+        def quantise_weight(name, raw, cast, rounded_w, pieces):
+            dst = rounded_w.rearrange("p (t m j) -> p m j t", t=PACK, j=PACK)
             for h in range(2):
-                cast(dst[:, 64 * h : 64 * (h + 1)], raw[h][:].rearrange("p j (m t) -> p m j t", t=PACK))
-            codes, scales, steps = quantise(name, grouped, pieces)
-            for step in steps:
-                step()
+                cast(dst[:, h * P // 2 : (h + 1) * P // 2], raw[h][:].rearrange("p j (m t) -> p m j t", t=PACK))
+            codes = sb(name + "_codes", [P, N], U32)
+            scales = sb(name + "_bytes", [P, N], U8)
+            width = N // pieces
+            for i in range(pieces):
+                cols = slice(i * width, (i + 1) * width)
+                nc.vector.quantize_mx(out=codes[:, cols].bitcast(FP8X4), scales=scales[:, cols], in_=rounded_w[:, PACK * cols.start : PACK * cols.stop])
             return codes, scales
 
-        def product(bank, lw, ls, t, rw, rs):
-            nc.tensor.matmul_mx(out=bank[:], lhsT=lw[:, t * P : (t + 1) * P].bitcast(FP8X4), lhsT_scale=ls[:, t * P : (t + 1) * P],
-                                rhs=rw[:].bitcast(FP8X4), rhs_scale=rs[:], start=True, stop=True)
+        def product(dst, left_codes, left_bytes, t, right_codes, right_bytes):
+            rows = slice(t * P, (t + 1) * P)
+            nc.tensor.matmul_mx(
+                out=dst,
+                lhsT=left_codes[:, rows].bitcast(FP8X4),
+                lhsT_scale=left_bytes[:, rows],
+                rhs=right_codes.bitcast(FP8X4),
+                rhs_scale=right_bytes,
+                start=True,
+                stop=True,
+            )
 
-        rounded = turn.tile([P, 2, 2048], BF16, name="rounded", align_bytes=64, offset=512)
-        w1_w, w1_s = weight("w1q", w1_raw, lambda dst, src: nc.scalar.activation(dst, src, ACT.Copy), rounded[:, 0, :], 4)
-        a_ps = [psum.tile([P, 512], F32, name=f"a_ps{t}", tag=f"last{t}") for t in range(PACK)]
+        rounded = turn.tile([P, 2, PACK * N], BF16, name="rounded", align_bytes=64, offset=512)
+        w1_codes, w1_bytes = quantise_weight("w1", w1_raw, lambda dst, src: nc.scalar.activation(dst, src, ACT.Copy), rounded[:, 0, :], PACK)
+        a_ps = [psum.tile([P, N], F32, name=f"a_ps{t}", tag=f"bank{t}") for t in range(PACK)]
         for t in range(PACK):
-            product(a_ps[t], w1_w, w1_s, t, xa_w, xa_s)
-        nc.vector.tensor_copy(xb_w[:], xw[:].indirect(l_two[:]))
-        w2_w, w2_s = weight("w2q", w2_raw, nc.vector.tensor_copy, rounded[:, 1, :], 1)
+            product(a_ps[t][:], w1_codes, w1_bytes, t, xa_codes[:], xa_bytes[:])
+        nc.vector.tensor_copy(xb_codes[:], x_codes[:].indirect(l_two[:]))
+        w2_codes, w2_bytes = quantise_weight("w2", w2_raw, nc.vector.tensor_copy, rounded[:, 1, :], 1)
+        b_ps = [psum.tile([P, N], F32, name=f"b_ps{t}") for t in range(PACK)]
+        for t in range(PACK):
+            product(b_ps[t][:], w2_codes, w2_bytes, t, xb_codes[:], xb_bytes[:])
 
-        b_ps = [psum.tile([P, 512], F32, name=f"b_ps{t}") for t in range(PACK)]
-        for t in range(PACK):
-            product(b_ps[t], w2_w, w2_s, t, xb_w, xb_s)
-        a_sb = per_tile("a_sb", 512)
-        npa = per_tile("npa", W)
-        pb = per_tile("pb", W)
-        z_all = sb("z_all", [P, PACK, 512], F32)
-        b_sb = per_tile("b_sb", 512)
-        st = per_tile("st", 1024)
-        su = per_tile("su", 1024)
-        su_all = sb("su_all", [P, PACK, 512], F32)
-        h5_all = sb("h5_all", [P, PACK, 512], F32)
+        a_sb = per_tile("a_sb", N)
+        minus_pa = per_tile("minus_pa", PAIRS)
+        pb = per_tile("pb", PAIRS)
+        z_all = sb("z_all", [P, PACK, N], F32)
+        b_sb = per_tile("b_sb", N)
+        st = per_tile("st", 2 * N)
+        su = per_tile("su", 2 * N)
+        su_all = sb("su_all", [P, PACK, N], F32)
 
         def leave_a(t):
             nc.scalar.activation(a_sb[t][:], a_ps[t][:], ACT.Copy, scale=gain_a[:, t : t + 1])
@@ -141,118 +150,133 @@ def tile_picked_kqliftthreeodds_none_p_kernel(tc, x_words, x_scales, w1, w2, ga,
         def leave_b(t):
             nc.scalar.activation(b_sb[t][:], b_ps[t][:], ACT.Copy, scale=gain_b[:, t : t + 1])
 
-        def pair_fetch(t):
-            nc.scalar.activation(npa[t][:], a_sb[t][:].indirect(l1[:]), ACT.Copy, scale=-1.0)
+        def fetch_pairs(t):
+            nc.scalar.activation(minus_pa[t][:], a_sb[t][:].indirect(l1[:]), ACT.Copy, scale=-1.0)
             nc.scalar.activation(pb[t][:], a_sb[t][:].indirect(l2[:]), ACT.Copy)
 
-        def put_first(t, dt, gap):
-            nc.vector.scalar_tensor_tensor(gap[:], npa[t][:], -0.5, pb[t][:], ALU.mult, ALU.subtract)
-            nc.vector.tensor_tensor(dt[:].indirect(l1[:]), pb[t][:], npa[t][:], ALU.add)
-            return dt, gap
-
-        def put_second(t, dt, gap, tag):
-            lift = sb(f"lift{t}", [P, W], F32, tag)
+        def put_pairs(t, dt, gap):
+            nc.vector.scalar_tensor_tensor(gap[:], minus_pa[t][:], -0.5, pb[t][:], ALU.mult, ALU.subtract)
+            nc.vector.tensor_tensor(dt[:].indirect(l1[:]), pb[t][:], minus_pa[t][:], ALU.add)
+            lift = sb(f"lift{t}", [P, PAIRS], F32)
             nc.vector.tensor_scalar(lift[:], gap[:], low[:, t : t + 1], high[:, t : t + 1], ALU.max, ALU.min)
             nc.vector.tensor_tensor(dt[:].indirect(l2[:]), pb[t][:], lift[:], ALU.add)
-            if t < PACK - 1:
+            if t < LAST:
                 nc.sync.dma_start(z_all[:, t, :], dt[:])
             else:
                 nc.vector.tensor_copy(z_all[:, t, :], dt[:])
 
-        def diff_stage(t):
+        def make_st(t):
             for h in range(2):
-                nc.scalar.activation(st[t][:, 512 + h * HALF : 512 + (h + 1) * HALF], b_sb[t][:].indirect(l3[:, 16 * h : 16 * h + 16]), ACT.Copy)
-            nc.vector.tensor_tensor(st[t][:, 0:512], b_sb[t][:], st[t][:, 512:1024], ALU.subtract)
+                nc.scalar.activation(st[t][:, N + h * HALF : N + (h + 1) * HALF], b_sb[t][:].indirect(half_list(l3, h)), ACT.Copy)
+            nc.vector.tensor_tensor(st[t][:, 0:N], b_sb[t][:], st[t][:, N : 2 * N], ALU.subtract)
 
-        def max_stage(t):
-            nc.scalar.activation(su[t][:, 512:1024], st[t][:].indirect(l4[:]), ACT.Copy)
-            nc.vector.tensor_tensor(su[t][:, 0:512], st[t][:, 0:512], su[t][:, 512:1024], ALU.max)
-            if t < PACK - 1:
-                nc.sync.dma_start(su_all[:, t, :], su[t][:, 0:512])
+        def make_su(t):
+            nc.scalar.activation(su[t][:, N : 2 * N], st[t][:].indirect(l4[:]), ACT.Copy)
+            nc.vector.tensor_tensor(su[t][:, 0:N], st[t][:, 0:N], su[t][:, N : 2 * N], ALU.max)
+            if t < PACK // 2:
+                nc.sync.dma_start(su_all[:, t, :], su[t][:, 0:N])
             else:
-                nc.vector.tensor_copy(su_all[:, t, :], su[t][:, 0:512])
+                nc.vector.tensor_copy(su_all[:, t, :], su[t][:, 0:N])
 
-        early = [turn.tile([P, 512], F32, name=f"dt{t}", align_bytes=64, offset=3072 * t + 1024) for t in range(PACK - 1)]
-        early_gap = [turn.tile([P, W], F32, name=f"gap{t}", align_bytes=64, offset=3072 * t) for t in range(PACK - 1)]
+        gap_bytes, dt_bytes = 4 * PAIRS, 4 * N
+        dt_first = [turn.tile([P, N], F32, name=f"dt{t}", align_bytes=64, offset=(gap_bytes + dt_bytes) * t + gap_bytes) for t in range(LAST)]
+        gap_first = [turn.tile([P, PAIRS], F32, name=f"gap{t}", align_bytes=64, offset=(gap_bytes + dt_bytes) * t) for t in range(LAST)]
         leave_a(0)
-        for t in range(PACK - 1):
+        for t in range(LAST):
             leave_a(t + 1)
-            pair_fetch(t)
-            put_second(t, *put_first(t, early[t], early_gap[t]), None)
+            fetch_pairs(t)
+            put_pairs(t, dt_first[t], gap_first[t])
         leave_b(0)
-        pair_fetch(PACK - 1)
+        fetch_pairs(LAST)
         for t in range(PACK):
-            if t + 1 < PACK:
+            if t < LAST:
                 leave_b(t + 1)
-            diff_stage(t)
-        max_stage(0)
-        last = put_first(PACK - 1, sb("dt3", [P, 512], F32, "st0"), sb("gap3", [P, W], F32, "b_sb0"))
-        for t in range(1, PACK):
-            max_stage(t)
-        put_second(PACK - 1, *last, "st3")
+            make_st(t)
+        put_pairs(LAST, sb("dt_last", [P, N], F32, on=f"b_sb{LAST}"), sb("gap_last", [P, PAIRS], F32, on="b_sb0"))
+        for t in range(PACK):
+            make_su(t)
 
-        z2_g = sb("z2_g", [P, 2048], BF16)
-        z2_w, z2_s, z2_steps = quantise("z2q", z2_g, 2)
-        z_g = sb("z_g", [P, 2048], BF16)
-        z_w, z_s, z_steps = quantise("zq", z_g, 2)
+        z2_codes = sb("z2_codes", [P, N], U32)
+        z2_bytes = sb("z2_bytes", [P, N], U8)
+        z_codes = sb("z_codes", [P, N], U32)
+        z_bytes = sb("z_bytes", [P, N], U8)
 
-        def sum_stage(h):
-            cols = slice(h * HALF, (h + 1) * HALF)
+        def quantise_z(h, cast, on):
+            z_rounded = sb(f"z_rounded{h}", [P, PACK * HALF], BF16, on=on)
+            cast(
+                z_rounded[:].rearrange("p (u m t) -> p m t u", u=2, t=PACK),
+                z_all[:].rearrange("p t (m u) -> p m t u", u=PACK)[:, :, :, 2 * h : 2 * h + 2],
+            )
+            nc.vector.quantize_mx(out=z_codes[:, half(h)].bitcast(FP8X4), scales=z_bytes[:, half(h)], in_=z_rounded[:])
+
+        def quantise_z2(h, on):
+            half_su5 = sb(f"half_su5_{h}", [P, PACK, HALF], F32)
+            z2_rounded = sb(f"z2_rounded{h}", [P, PACK * HALF], BF16, on=on)
             for t in range(PACK):
-                nc.scalar.activation(h5_all[:, t, cols], su[t][:].indirect(l5[:, 16 * h : 16 * h + 16]), ACT.Copy, scale=0.5)
+                nc.scalar.activation(half_su5[:, t, :], su[t][:].indirect(half_list(l5, h)), ACT.Copy, scale=0.5)
             nc.vector.tensor_tensor(
-                z2_g[:, PACK * h * HALF : PACK * (h + 1) * HALF].rearrange("p (c i t) -> p c t i", i=4, t=PACK),
-                su_all[:, :, cols].rearrange("p t (c i) -> p c t i", i=4),
-                h5_all[:, :, cols].rearrange("p t (c i) -> p c t i", i=4),
-                ALU.add)
-            z2_steps[h]()
+                z2_rounded[:].rearrange("p (c i t) -> p c t i", i=2, t=PACK),
+                su_all[:, :, half(h)].rearrange("p t (c i) -> p c t i", i=2),
+                half_su5[:].rearrange("p t (c i) -> p c t i", i=2),
+                ALU.add,
+            )
+            nc.vector.quantize_mx(out=z2_codes[:, half(h)].bitcast(FP8X4), scales=z2_bytes[:, half(h)], in_=z2_rounded[:])
 
-        z_dst = z_g[:].rearrange("p (u m t) -> p m t u", u=PACK, t=PACK)
-        z_src = z_all[:].rearrange("p t (m u) -> p m t u", u=PACK)
-        sum_stage(0)
-        sum_stage(1)
-        nc.scalar.copy(z_dst[:, :, :, 0:2], z_src[:, :, :, 0:2])
-        z_steps[0]()
-        nc.vector.tensor_copy(z_dst[:, :, :, 2:4], z_src[:, :, :, 2:4])
-        z_steps[1]()
-
-        s_ps = [psum.tile([P, 512], F32, name=f"s_ps{t}", tag=f"last{t}") for t in range(PACK)]
+        s_ps = [psum.tile([P, N], F32, name=f"s_ps{t}", tag=f"bank{t}") for t in range(PACK)]
         shift = per_tile("shift", 1)
-        ex2 = per_tile("ex2", 512)
-        g7 = per_tile("g7", 512)
-        num = per_tile("num", 512)
-        res = per_tile("res", 512)
-        out_rows = out.rearrange("(p u) v -> p u v", u=PACK)
-        for t in range(PACK):
-            product(s_ps[t], z_w, z_s, t, z2_w, z2_s)
-        for t in range(PACK):
-            nc.scalar.activation(shift[t][:], s_ps[t][:, 0:1], ACT.Copy, scale=-0.03125)
-            nc.scalar.activation(su[t][:, 0:512], s_ps[t][:], ACT.Exp, bias=shift[t][:], scale=0.03125)
-            if t < 2:
-                nc.vector.tensor_copy(ex2[t][:], su[t][:, 0:512])
-            else:
-                nc.sync.dma_start(ex2[t][:], su[t][:, 0:512])
-            nc.vector.tensor_tensor(num[t][:], su[t][:].indirect(l6[:]), ex2[t][:], ALU.add)
 
-        def below(t, den):
-            nc.scalar.activation(g7[t][:], su[t][:].indirect(l7[:]), ACT.Copy)
-            nc.vector.tensor_tensor(den[:], su[t][:].indirect(l8[:]), g7[t][:], ALU.add)
+        def score(t, cols):
+            product(s_ps[t][:, cols], z_codes, z_bytes, t, z2_codes[:, cols], z2_bytes[:, cols])
+
+        early, late = range(PACK // 2), range(PACK // 2, PACK)
+        quantise_z(0, nc.vector.tensor_copy, on=None)
+        quantise_z2(0, on=None)
+        for t in early:
+            score(t, half(0))
+        quantise_z2(1, on="z_rounded0")
+        for t in early:
+            nc.vector.tensor_scalar(shift[t][:], s_ps[t][:, 0:1], -EXP_SCALE, 0.0, ALU.mult, ALU.add)
+            score(t, half(1))
+        quantise_z(1, nc.scalar.copy, on=f"su{LAST}")
+        for t in late:
+            score(t, slice(0, N))
+
+        ex = st
+        ex_copy = per_tile("ex_copy", N)
+        ex7 = per_tile("ex7", N)
+        num = per_tile("num", N)
+        res = per_tile("res", N)
+        out_rows = out.rearrange("(p t) v -> p t v", t=PACK)
+        for t in range(PACK):
+            if t in late:
+                nc.scalar.activation(shift[t][:], s_ps[t][:, 0:1], ACT.Copy, scale=-EXP_SCALE)
+            nc.scalar.activation(ex[t][:, 0:N], s_ps[t][:], ACT.Exp, bias=shift[t][:], scale=EXP_SCALE)
+            if t in early:
+                nc.vector.tensor_copy(ex_copy[t][:], ex[t][:, 0:N])
+            else:
+                nc.sync.dma_start(ex_copy[t][:], ex[t][:, 0:N])
+            nc.vector.tensor_tensor(num[t][:], ex[t][:].indirect(l6[:]), ex_copy[t][:], ALU.add)
+
+        def make_den(t, den):
+            nc.vector.tensor_tensor(den[:], ex[t][:].indirect(l8[:]), ex7[t][:], ALU.add)
             return den
 
-        def finish(t, den, pieces=1):
+        def finish(t, den, pieces):
             nc.scalar.activation(num[t][:], num[t][:], ACT.Ln)
             for i in range(pieces):
-                cols = slice(i * 512 // pieces, (i + 1) * 512 // pieces)
+                cols = slice(i * N // pieces, (i + 1) * N // pieces)
                 nc.scalar.activation(den[:, cols], den[:, cols], ACT.Ln)
                 nc.vector.tensor_tensor(res[t][:, cols], num[t][:, cols], den[:, cols], ALU.subtract)
                 nc.sync.dma_start(out_rows[:, t, cols], res[t][:, cols])
 
-        dens = [below(t, sb(f"den{t}", [P, 512], F32)) for t in range(PACK - 1)]
-        nc.scalar.activation(g7[3][:, 0:HALF], su[3][:].indirect(l7[:, 0:16]), ACT.Copy)
-        nc.vector.tensor_copy(g7[3][:, HALF:512], su[3][:].indirect(l7[:, 16:32]))
-        finish(0, dens[0])
-        den3 = sb("den3", [P, 512], F32, "den0")
-        nc.vector.tensor_tensor(den3[:], su[3][:].indirect(l8[:]), g7[3][:], ALU.add)
-        finish(1, dens[1])
-        finish(2, dens[2])
-        finish(3, den3, 2)
+        dens = []
+        for t in range(LAST):
+            nc.scalar.activation(ex7[t][:], ex[t][:].indirect(l7[:]), ACT.Copy)
+            dens.append(make_den(t, sb(f"den{t}", [P, N], F32)))
+        nc.scalar.activation(ex7[LAST][:, half(0)], ex[LAST][:].indirect(half_list(l7, 0)), ACT.Copy)
+        nc.vector.tensor_copy(ex7[LAST][:, half(1)], ex[LAST][:].indirect(half_list(l7, 1)))
+        finish(0, dens[0], 1)
+        den_last = make_den(LAST, sb("den_last", [P, N], F32, on="den0"))
+        for t in range(1, LAST):
+            finish(t, dens[t], 1)
+        finish(LAST, den_last, 2)

from contextlib import ExitStack

import concourse.mybir as mybir

T = 2048
N = 512
PAIRS = 256
FLOPS = 3 * 2 * N * N * N

F32 = mybir.dt.float32
BF16 = mybir.dt.bfloat16
I32 = mybir.dt.int32
U32 = mybir.dt.uint32
U16 = mybir.dt.uint16
U8 = mybir.dt.uint8
FP8X4 = mybir.dt.float8_e4m3fn_x4
ALU = mybir.AluOpType
ACT = mybir.ActivationFunctionType

P = 128
PACK = 4
LAST = PACK - 1
HALF = N // 2
GROUP = 16
NO_BOUND = 3.0e38
EXP_SCALE = 0.5 * 0.0625


def tile_picked_kqliftthreeodds_none_p_kernel(tc, x_words, x_scales, w1, w2, ga, gb, offs, two, n1, n2, n3, n4, n5, n6, n7, n8, out):
    nc = tc.nc
    with ExitStack() as ctx:
        keep = ctx.enter_context(tc.tile_pool(name="keep", bufs=1))
        turn = ctx.enter_context(tc.tile_pool(name="turn", bufs=1))
        psum = ctx.enter_context(tc.psum_pool(name="psum", bufs=1))

        def sb(name, shape, dtype, on=None):
            return keep.tile(shape, dtype, name=name, tag=on or name, align_bytes=64)

        def per_tile(name, width):
            return [sb(f"{name}{t}", [P, width], F32) for t in range(PACK)]

        def half(h):
            return slice(h * HALF, (h + 1) * HALF)

        def half_list(tile, h):
            return tile[:, h * HALF // GROUP : (h + 1) * HALF // GROUP]

        def load_list(name, src):
            tile = sb(name, list(src.shape), U16)
            nc.sync.dma_start(tile[:], src)
            return tile

        def load_weight_half(name, w, h):
            tile = sb(name, [P, PACK, HALF], F32)
            nc.sync.dma_start(tile[:], w.rearrange("(p j) c -> p j c", j=PACK)[:, :, half(h)])
            return tile

        x_bytes = sb("x_bytes", [P, T], U8)
        nc.gpsimd.memset(x_bytes[:].bitcast(I32), 0)
        l_offs = load_list("l_offs", offs)
        l_two = load_list("l_two", two)
        w1_raw = [load_weight_half("w1_raw0", w1, 0)]
        for q in range(4):
            nc.sync.dma_start(x_bytes[32 * q : 32 * q + 4, :].bitcast(I32), x_scales[0, 4 * q : 4 * q + 4, :].bitcast(I32))
        w1_raw.append(load_weight_half("w1_raw1", w1, 1))
        x_codes = sb("x_codes", [P, T], U32)
        nc.sync.dma_start(x_codes[:].bitcast(I32), x_words[0].rearrange("p n t -> p (n t)").bitcast(I32))
        ga_sb = sb("ga_sb", [P, PACK], F32)
        gb_sb = sb("gb_sb", [P, PACK], F32)
        nc.sync.dma_start(ga_sb[:], ga.rearrange("(p t) o -> p (t o)", t=PACK))
        nc.sync.dma_start(gb_sb[:], gb.rearrange("(p t) o -> p (t o)", t=PACK))
        l1 = load_list("l1", n1)
        l2 = load_list("l2", n2)
        w2_raw = [load_weight_half(f"w2_raw{h}", w2, h) for h in range(2)]
        l3 = load_list("l3", n3)
        l4 = load_list("l4", n4)
        l5 = load_list("l5", n5)
        l6 = load_list("l6", n6)
        l7 = load_list("l7", n7)
        l8 = load_list("l8", n8)

        minus_two = sb("minus_two", [P, PACK], F32)
        sign_b = sb("sign_b", [P, PACK], F32)
        gain_a = sb("gain_a", [P, PACK], F32)
        gain_b = sb("gain_b", [P, PACK], F32)
        low = sb("low", [P, PACK], F32)
        high = sb("high", [P, PACK], F32)
        nc.gpsimd.tensor_scalar(minus_two[:], gb_sb[:], 0.0, -2.0, ALU.is_lt, ALU.mult)
        nc.gpsimd.tensor_scalar(sign_b[:], minus_two[:], 1.0, 1.0, ALU.mult, ALU.add)
        nc.gpsimd.tensor_tensor(gain_a[:], ga_sb[:], sign_b[:], ALU.mult)
        nc.gpsimd.tensor_tensor(gain_b[:], gb_sb[:], sign_b[:], ALU.mult)
        nc.gpsimd.tensor_scalar(high[:], gain_a[:], 0.0, NO_BOUND, ALU.is_ge, ALU.mult)
        nc.gpsimd.tensor_scalar(low[:], gain_a[:], 0.0, -NO_BOUND, ALU.is_lt, ALU.mult)

        xa_bytes = sb("xa_bytes", [P, N], U8)
        xb_bytes = sb("xb_bytes", [P, N], U8)
        xa_codes = sb("xa_codes", [P, N], U32)
        xb_codes = sb("xb_codes", [P, N], U32)
        nc.vector.tensor_copy(xa_bytes[:], x_bytes[:].indirect(l_offs[:]))
        nc.vector.tensor_copy(xb_bytes[:], x_bytes[:].indirect(l_two[:]))
        nc.vector.tensor_copy(xa_codes[:], x_codes[:].indirect(l_offs[:]))

        def quantise_weight(name, raw, cast, rounded_w, pieces):
            dst = rounded_w.rearrange("p (t m j) -> p m j t", t=PACK, j=PACK)
            for h in range(2):
                cast(dst[:, h * P // 2 : (h + 1) * P // 2], raw[h][:].rearrange("p j (m t) -> p m j t", t=PACK))
            codes = sb(name + "_codes", [P, N], U32)
            scales = sb(name + "_bytes", [P, N], U8)
            width = N // pieces
            for i in range(pieces):
                cols = slice(i * width, (i + 1) * width)
                nc.vector.quantize_mx(out=codes[:, cols].bitcast(FP8X4), scales=scales[:, cols], in_=rounded_w[:, PACK * cols.start : PACK * cols.stop])
            return codes, scales

        def product(dst, left_codes, left_bytes, t, right_codes, right_bytes):
            rows = slice(t * P, (t + 1) * P)
            nc.tensor.matmul_mx(
                out=dst,
                lhsT=left_codes[:, rows].bitcast(FP8X4),
                lhsT_scale=left_bytes[:, rows],
                rhs=right_codes.bitcast(FP8X4),
                rhs_scale=right_bytes,
                start=True,
                stop=True,
            )

        rounded = turn.tile([P, 2, PACK * N], BF16, name="rounded", align_bytes=64, offset=512)
        w1_codes, w1_bytes = quantise_weight("w1", w1_raw, lambda dst, src: nc.scalar.activation(dst, src, ACT.Copy), rounded[:, 0, :], PACK)
        a_ps = [psum.tile([P, N], F32, name=f"a_ps{t}", tag=f"bank{t}") for t in range(PACK)]
        for t in range(PACK):
            product(a_ps[t][:], w1_codes, w1_bytes, t, xa_codes[:], xa_bytes[:])
        nc.vector.tensor_copy(xb_codes[:], x_codes[:].indirect(l_two[:]))
        w2_codes, w2_bytes = quantise_weight("w2", w2_raw, nc.vector.tensor_copy, rounded[:, 1, :], 1)
        b_ps = [psum.tile([P, N], F32, name=f"b_ps{t}") for t in range(PACK)]
        for t in range(PACK):
            product(b_ps[t][:], w2_codes, w2_bytes, t, xb_codes[:], xb_bytes[:])

        a_sb = per_tile("a_sb", N)
        minus_pa = per_tile("minus_pa", PAIRS)
        pb = per_tile("pb", PAIRS)
        z_all = sb("z_all", [P, PACK, N], F32)
        b_sb = per_tile("b_sb", N)
        st = per_tile("st", 2 * N)
        su = per_tile("su", 2 * N)
        su_all = sb("su_all", [P, PACK, N], F32)

        def leave_a(t):
            nc.scalar.activation(a_sb[t][:], a_ps[t][:], ACT.Copy, scale=gain_a[:, t : t + 1])

        def leave_b(t):
            nc.scalar.activation(b_sb[t][:], b_ps[t][:], ACT.Copy, scale=gain_b[:, t : t + 1])

        def fetch_pairs(t):
            nc.scalar.activation(minus_pa[t][:], a_sb[t][:].indirect(l1[:]), ACT.Copy, scale=-1.0)
            nc.scalar.activation(pb[t][:], a_sb[t][:].indirect(l2[:]), ACT.Copy)

        def put_pairs(t, dt, gap):
            nc.vector.scalar_tensor_tensor(gap[:], minus_pa[t][:], -0.5, pb[t][:], ALU.mult, ALU.subtract)
            nc.vector.tensor_tensor(dt[:].indirect(l1[:]), pb[t][:], minus_pa[t][:], ALU.add)
            lift = sb(f"lift{t}", [P, PAIRS], F32)
            nc.vector.tensor_scalar(lift[:], gap[:], low[:, t : t + 1], high[:, t : t + 1], ALU.max, ALU.min)
            nc.vector.tensor_tensor(dt[:].indirect(l2[:]), pb[t][:], lift[:], ALU.add)
            if t < LAST:
                nc.sync.dma_start(z_all[:, t, :], dt[:])
            else:
                nc.vector.tensor_copy(z_all[:, t, :], dt[:])

        def make_st(t):
            for h in range(2):
                nc.scalar.activation(st[t][:, N + h * HALF : N + (h + 1) * HALF], b_sb[t][:].indirect(half_list(l3, h)), ACT.Copy)
            nc.vector.tensor_tensor(st[t][:, 0:N], b_sb[t][:], st[t][:, N : 2 * N], ALU.subtract)

        def make_su(t):
            nc.scalar.activation(su[t][:, N : 2 * N], st[t][:].indirect(l4[:]), ACT.Copy)
            nc.vector.tensor_tensor(su[t][:, 0:N], st[t][:, 0:N], su[t][:, N : 2 * N], ALU.max)
            if t < PACK // 2:
                nc.sync.dma_start(su_all[:, t, :], su[t][:, 0:N])
            else:
                nc.vector.tensor_copy(su_all[:, t, :], su[t][:, 0:N])

        gap_bytes, dt_bytes = 4 * PAIRS, 4 * N
        dt_first = [turn.tile([P, N], F32, name=f"dt{t}", align_bytes=64, offset=(gap_bytes + dt_bytes) * t + gap_bytes) for t in range(LAST)]
        gap_first = [turn.tile([P, PAIRS], F32, name=f"gap{t}", align_bytes=64, offset=(gap_bytes + dt_bytes) * t) for t in range(LAST)]
        leave_a(0)
        for t in range(LAST):
            leave_a(t + 1)
            fetch_pairs(t)
            put_pairs(t, dt_first[t], gap_first[t])
        leave_b(0)
        fetch_pairs(LAST)
        for t in range(PACK):
            if t < LAST:
                leave_b(t + 1)
            make_st(t)
        put_pairs(LAST, sb("dt_last", [P, N], F32, on=f"b_sb{LAST}"), sb("gap_last", [P, PAIRS], F32, on="b_sb0"))
        for t in range(PACK):
            make_su(t)

        z2_codes = sb("z2_codes", [P, N], U32)
        z2_bytes = sb("z2_bytes", [P, N], U8)
        z_codes = sb("z_codes", [P, N], U32)
        z_bytes = sb("z_bytes", [P, N], U8)

        def quantise_z(h, cast, on):
            z_rounded = sb(f"z_rounded{h}", [P, PACK * HALF], BF16, on=on)
            cast(
                z_rounded[:].rearrange("p (u m t) -> p m t u", u=2, t=PACK),
                z_all[:].rearrange("p t (m u) -> p m t u", u=PACK)[:, :, :, 2 * h : 2 * h + 2],
            )
            nc.vector.quantize_mx(out=z_codes[:, half(h)].bitcast(FP8X4), scales=z_bytes[:, half(h)], in_=z_rounded[:])

        def quantise_z2(h, on):
            half_su5 = sb(f"half_su5_{h}", [P, PACK, HALF], F32)
            z2_rounded = sb(f"z2_rounded{h}", [P, PACK * HALF], BF16, on=on)
            for t in range(PACK):
                nc.scalar.activation(half_su5[:, t, :], su[t][:].indirect(half_list(l5, h)), ACT.Copy, scale=0.5)
            nc.vector.tensor_tensor(
                z2_rounded[:].rearrange("p (c i t) -> p c t i", i=2, t=PACK),
                su_all[:, :, half(h)].rearrange("p t (c i) -> p c t i", i=2),
                half_su5[:].rearrange("p t (c i) -> p c t i", i=2),
                ALU.add,
            )
            nc.vector.quantize_mx(out=z2_codes[:, half(h)].bitcast(FP8X4), scales=z2_bytes[:, half(h)], in_=z2_rounded[:])

        s_ps = [psum.tile([P, N], F32, name=f"s_ps{t}", tag=f"bank{t}") for t in range(PACK)]
        shift = per_tile("shift", 1)

        def score(t, cols):
            product(s_ps[t][:, cols], z_codes, z_bytes, t, z2_codes[:, cols], z2_bytes[:, cols])

        early, late = range(PACK // 2), range(PACK // 2, PACK)
        quantise_z(0, nc.vector.tensor_copy, on=None)
        quantise_z2(0, on=None)
        for t in early:
            score(t, half(0))
        quantise_z2(1, on="z_rounded0")
        for t in early:
            nc.vector.tensor_scalar(shift[t][:], s_ps[t][:, 0:1], -EXP_SCALE, 0.0, ALU.mult, ALU.add)
            score(t, half(1))
        quantise_z(1, nc.scalar.copy, on=f"su{LAST}")
        for t in late:
            score(t, slice(0, N))

        ex = st
        ex_copy = per_tile("ex_copy", N)
        ex7 = per_tile("ex7", N)
        num = per_tile("num", N)
        res = per_tile("res", N)
        out_rows = out.rearrange("(p t) v -> p t v", t=PACK)
        for t in range(PACK):
            if t in late:
                nc.scalar.activation(shift[t][:], s_ps[t][:, 0:1], ACT.Copy, scale=-EXP_SCALE)
            nc.scalar.activation(ex[t][:, 0:N], s_ps[t][:], ACT.Exp, bias=shift[t][:], scale=EXP_SCALE)
            if t in early:
                nc.vector.tensor_copy(ex_copy[t][:], ex[t][:, 0:N])
            else:
                nc.sync.dma_start(ex_copy[t][:], ex[t][:, 0:N])
            nc.vector.tensor_tensor(num[t][:], ex[t][:].indirect(l6[:]), ex_copy[t][:], ALU.add)

        def make_den(t, den):
            nc.vector.tensor_tensor(den[:], ex[t][:].indirect(l8[:]), ex7[t][:], ALU.add)
            return den

        def finish(t, den, pieces):
            nc.scalar.activation(num[t][:], num[t][:], ACT.Ln)
            for i in range(pieces):
                cols = slice(i * N // pieces, (i + 1) * N // pieces)
                nc.scalar.activation(den[:, cols], den[:, cols], ACT.Ln)
                nc.vector.tensor_tensor(res[t][:, cols], num[t][:, cols], den[:, cols], ALU.subtract)
                nc.sync.dma_start(out_rows[:, t, cols], res[t][:, cols])

        dens = []
        for t in range(LAST):
            nc.scalar.activation(ex7[t][:], ex[t][:].indirect(l7[:]), ACT.Copy)
            dens.append(make_den(t, sb(f"den{t}", [P, N], F32)))
        nc.scalar.activation(ex7[LAST][:, half(0)], ex[LAST][:].indirect(half_list(l7, 0)), ACT.Copy)
        nc.vector.tensor_copy(ex7[LAST][:, half(1)], ex[LAST][:].indirect(half_list(l7, 1)))
        finish(0, dens[0], 1)
        den_last = make_den(LAST, sb("den_last", [P, N], F32, on="den0"))
        for t in range(1, LAST):
            finish(t, dens[t], 1)
        finish(LAST, den_last, 2)
